import numpy as np
import ml_dtypes


def mxq(x, axis, fmt="e4m3"):
    dtype, down = {"e4m3": (ml_dtypes.float8_e4m3fn, 7), "e5m2": (ml_dtypes.float8_e5m2, 14)}[fmt]
    v = np.moveaxis(np.asarray(x, np.float32).astype(ml_dtypes.bfloat16).astype(np.float64), axis, -1)
    blocks = v.reshape(v.shape[:-1] + (-1, 32))
    amax = np.abs(blocks).max(-1, keepdims=True)
    byte = np.maximum(np.where(amax > 0, np.frexp(amax)[1] - 1 + 127, 0) - down, 1)
    scale = np.exp2(byte - 127.0)
    codes = (blocks / scale).astype(np.float32).astype(dtype).astype(np.float64)
    return np.moveaxis((codes * scale).reshape(v.shape), -1, axis)


WIDE = False


def mx_kscale(k):
    if not WIDE:
        return np.ones(k)
    levels = np.array([10, -10, 5, -5, 0])
    if k % 512:
        return np.exp2(np.random.permutation(np.resize(levels, k // 32))).repeat(32)
    a = np.empty((k // 512, 16))
    for p in range(k // 512):
        a[p, :8] = np.random.permutation(np.resize(levels, 8))
        for g in range(8):
            far = levels[np.abs(levels - a[p, g]) >= 10]
            a[p, g + 8] = far[np.random.randint(len(far))]
    return np.exp2(a.ravel()).repeat(32)


def f64(x):
    return np.asarray(x).astype(np.float64)


def striped8(idx):
    return np.concatenate([x.reshape(-1, 16).T for x in idx]).astype(np.uint16)


def runs(offs, k):
    lists = np.stack([offs[16 * r : 16 * r + 16].T.reshape(-1) for r in range(8)]).astype(np.int64)
    return lists[np.arange(k) % 512 // 64]


def pack_weight(w):
    k, n = w.shape
    w = f64(np.asarray(w, np.float32).astype(ml_dtypes.bfloat16)).reshape(k // 32, 32, n)
    amax = np.abs(w).max(1)
    byte = np.clip(np.where(amax > 0, np.frexp(amax)[1] - 1 + 127 - 7, 1), 1, 254)
    scaled = (w * np.exp2(127.0 - byte)[:, None, :]).reshape(k, n).astype(np.float32)
    words = np.ascontiguousarray(scaled.reshape(k // 512, 128, 4, n).transpose(0, 1, 3, 2)).astype(ml_dtypes.float8_e4m3fn).view(np.uint8)
    return words, np.ascontiguousarray(byte.astype(np.uint8).reshape(k // 512, 16, n))


def unpack_weight(words, scales):
    g, p, n, _ = words.shape
    vals = np.ascontiguousarray(words).view(ml_dtypes.float8_e4m3fn).astype(np.float64) * np.repeat(np.exp2(scales.astype(np.float64) - 127.0), 8, axis=1)[..., None]
    return vals.transpose(0, 1, 3, 2).reshape(g * 512, n)


K, T, S, N = 512, 2048, 512, 128
P = 2 ** 7


def setup_inputs():
    n = np.random.standard_normal
    s = mx_kscale(K)[:, None]
    packed_xT = pack_weight(n((K, T)) * s)
    return {
        "x_words": packed_xT[0],
        "x_scales": packed_xT[1],
        "w1": (n((K, N)) / np.sqrt(K) / s).astype(np.float32),
        "prior": np.tile(0.5 * np.random.standard_normal(S), (P, 1)).astype(np.float32),
        "offs": striped8(np.random.randint(0, T, (8, S))),
    }


def reference(x_words, x_scales, w1, prior, offs):
    xq = unpack_weight(x_words, x_scales)[np.arange(K)[:, None], runs(offs, K)]
    y = mxq(f64(w1), 0, "e4m3").T @ xq
    yp = y + f64(prior)[:1]
    e = np.exp(yp - yp.max(axis=1, keepdims=True))
    return e / e.sum(axis=1, keepdims=True)

@@ -1,0 +1,93 @@
+from contextlib import ExitStack
+
+import concourse.mybir as mybir
+
+K, T, S, N = 512, 2048, 512, 128
+FLOPS = 2 * K * N * S
+
+F32 = mybir.dt.float32
+BF16 = mybir.dt.bfloat16
+I32 = mybir.dt.int32
+U32 = mybir.dt.uint32
+U16 = mybir.dt.uint16
+U8 = mybir.dt.uint8
+FP8X4 = mybir.dt.float8_e4m3fn_x4
+ALU = mybir.AluOpType
+ACT = mybir.ActivationFunctionType
+
+P = 128
+PACK = 4
+HALF = S // 2
+
+
+def tile_picked_phrank_none_p_kernel(tc, x_words, x_scales, w1, prior, offs, out):
+    nc = tc.nc
+    with ExitStack() as ctx:
+        keep = ctx.enter_context(tc.tile_pool(name="keep", bufs=1))
+        psum = ctx.enter_context(tc.psum_pool(name="psum", bufs=1))
+
+        offsets = keep.tile([P, S // 16], U16, name="offsets")
+        nc.sync.dma_start(offsets[:], offs)
+
+        byte_table = keep.tile([P, T], U8, name="byte_table")
+        nc.vector.memset(byte_table[:].bitcast(I32), 0)
+        nc.scalar.dma_start(byte_table[0:P:8, :].bitcast(I32), x_scales[0].bitcast(I32))
+        plane = keep.tile([P, S], U8, name="plane", align_bytes=64)
+        nc.vector.memset(plane[:].bitcast(I32), 0)
+
+        w_raw = keep.tile([P, PACK, N], F32, name="w_raw")
+        nc.sync.dma_start(w_raw[:], w1.rearrange("(p j) m -> p j m", j=PACK))
+
+        word_table = keep.tile([P, T], I32, name="word_table")
+        nc.sync.dma_start(word_table[:], x_words[0].rearrange("p c r -> p (c r)").bitcast(I32))
+
+        prior_sb = keep.tile([P, S], F32, name="prior_sb")
+        nc.sync.dma_start(prior_sb[:], prior)
+
+        w_grouped = keep.tile([P, N, PACK], BF16, name="w_grouped", align_bytes=64)
+        nc.scalar.copy(w_grouped[:], w_raw[:].rearrange("p j m -> p m j"))
+
+        picked_bytes = keep.tile([P, S], U8, name="picked_bytes", align_bytes=64)
+        nc.vector.tensor_copy(picked_bytes[:], byte_table[:].indirect(offsets[:]))
+        for q in range(4):
+            queue = nc.scalar if q % 2 else nc.sync
+            queue.dma_start(plane[32 * q : 32 * q + 4, :].bitcast(I32), picked_bytes[32 * q : 32 * q + 32 : 8, :].bitcast(I32))
+
+        w_codes = keep.tile([P, N], U32, name="w_codes", align_bytes=64)
+        w_scales = keep.tile([P, N], U8, name="w_scales", align_bytes=64)
+        nc.vector.quantize_mx(out=w_codes[:].bitcast(FP8X4), scales=w_scales[:], in_=w_grouped[:].rearrange("p m j -> p (m j)"))
+
+        scores = []
+        for h in range(2):
+            cols = slice(h * HALF // 16, (h + 1) * HALF // 16)
+            picked_words = keep.tile([P, HALF], U32, name=f"picked_words{h}", align_bytes=64)
+            nc.vector.tensor_copy(picked_words[:], word_table[:].bitcast(U32).indirect(offsets[:, cols]))
+            acc = psum.tile([P, HALF], F32, name=f"acc{h}")
+            nc.tensor.matmul_mx(
+                out=acc[:],
+                lhsT=w_codes[:].bitcast(FP8X4),
+                lhsT_scale=w_scales[:],
+                rhs=picked_words[:].bitcast(FP8X4),
+                rhs_scale=plane[:, h * HALF : (h + 1) * HALF],
+                start=True,
+                stop=True,
+            )
+            scores.append(acc)
+
+        z = keep.tile([P, S], F32, name="z")
+        for h in range(2):
+            cols = slice(h * HALF, (h + 1) * HALF)
+            nc.vector.tensor_tensor(z[:, cols], scores[h][:], prior_sb[:, cols], ALU.add)
+        neg_max = keep.tile([P, 1], F32, name="neg_max")
+        nc.vector.tensor_reduce(neg_max[:], z[:], mybir.AxisListType.X, ALU.max, negate=True)
+
+        e_sb = keep.tile([P, S], F32, name="e_sb")
+        total = keep.tile([P, 1], F32, name="total")
+        nc.scalar.activation(e_sb[:], z[:], ACT.Exp, bias=neg_max[:], scale=1.0, accum_out=total[:])
+        inv = keep.tile([P, 1], F32, name="inv")
+        nc.vector.reciprocal(inv[:], total[:])
+        for h, queue in enumerate((nc.sync, nc.scalar)):
+            cols = slice(h * HALF, (h + 1) * HALF)
+            res = keep.tile([P, HALF], F32, name=f"res{h}")
+            nc.vector.tensor_scalar(res[:], e_sb[:, cols], inv[:], None, ALU.mult)
+            queue.dma_start(out[:, cols], res[:])

@@ -27,11 +27,10 @@ def tile_picked_phrank_none_p_kernel(tc, x_words, x_scales, w1, prior, offs, out
         psum = ctx.enter_context(tc.psum_pool(name="psum", bufs=1))
 
         offsets = keep.tile([P, S // 16], U16, name="offsets")
-        nc.sync.dma_start(offsets[:], offs)
 
         byte_table = keep.tile([P, T], U8, name="byte_table")
-        nc.vector.memset(byte_table[:].bitcast(I32), 0)
-        nc.scalar.dma_start(byte_table[0:P:8, :].bitcast(I32), x_scales[0].bitcast(I32))
+        nc.sync.dma_start(byte_table[:].bitcast(I32), x_scales[0].bitcast(I32).unsqueeze(1).to_broadcast([16, 8, T // 4]))
+        nc.sync.dma_start(offsets[:], offs)
         plane = keep.tile([P, S], U8, name="plane", align_bytes=64)
         nc.vector.memset(plane[:].bitcast(I32), 0)
 
@@ -45,7 +44,7 @@ def tile_picked_phrank_none_p_kernel(tc, x_words, x_scales, w1, prior, offs, out
         nc.sync.dma_start(prior_sb[:], prior)
 
         w_grouped = keep.tile([P, N, PACK], BF16, name="w_grouped", align_bytes=64)
-        nc.scalar.copy(w_grouped[:], w_raw[:].rearrange("p j m -> p m j"))
+        nc.vector.tensor_copy(w_grouped[:], w_raw[:].rearrange("p j m -> p m j"))
 
         picked_bytes = keep.tile([P, S], U8, name="picked_bytes", align_bytes=64)
         nc.vector.tensor_copy(picked_bytes[:], byte_table[:].indirect(offsets[:]))

@@ -29,7 +29,8 @@ def tile_picked_phrank_none_p_kernel(tc, x_words, x_scales, w1, prior, offs, out
         offsets = keep.tile([P, S // 16], U16, name="offsets")
 
         byte_table = keep.tile([P, T], U8, name="byte_table")
-        nc.sync.dma_start(byte_table[:].bitcast(I32), x_scales[0].bitcast(I32).unsqueeze(1).to_broadcast([16, 8, T // 4]))
+        nc.vector.memset(byte_table[:].bitcast(I32), 0)
+        nc.sync.dma_start(byte_table[0:P:8, :].bitcast(I32), x_scales[0].bitcast(I32))
         nc.sync.dma_start(offsets[:], offs)
         plane = keep.tile([P, S], U8, name="plane", align_bytes=64)
         nc.vector.memset(plane[:].bitcast(I32), 0)
@@ -44,7 +45,7 @@ def tile_picked_phrank_none_p_kernel(tc, x_words, x_scales, w1, prior, offs, out
         nc.sync.dma_start(prior_sb[:], prior)
 
         w_grouped = keep.tile([P, N, PACK], BF16, name="w_grouped", align_bytes=64)
-        nc.vector.tensor_copy(w_grouped[:], w_raw[:].rearrange("p j m -> p m j"))
+        nc.scalar.copy(w_grouped[:], w_raw[:].rearrange("p j m -> p m j"))
 
         picked_bytes = keep.tile([P, S], U8, name="picked_bytes", align_bytes=64)
         nc.vector.tensor_copy(picked_bytes[:], byte_table[:].indirect(offsets[:]))
@@ -73,16 +74,16 @@ def tile_picked_phrank_none_p_kernel(tc, x_words, x_scales, w1, prior, offs, out
             )
             scores.append(acc)
 
-        z = keep.tile([P, S], F32, name="z")
-        for h in range(2):
-            cols = slice(h * HALF, (h + 1) * HALF)
-            nc.vector.tensor_tensor(z[:, cols], scores[h][:], prior_sb[:, cols], ALU.add)
+        z = keep.tile([P, S + 1], F32, name="z")
         neg_max = keep.tile([P, 1], F32, name="neg_max")
-        nc.vector.tensor_reduce(neg_max[:], z[:], mybir.AxisListType.X, ALU.max, negate=True)
+        nc.vector.tensor_tensor(z[:, :HALF], scores[0][:], prior_sb[:, :HALF], ALU.add)
+        nc.vector.tensor_reduce(z[:, S:], z[:, :HALF], mybir.AxisListType.X, ALU.max)
+        nc.vector.tensor_tensor(z[:, HALF:S], scores[1][:], prior_sb[:, HALF:], ALU.add)
+        nc.vector.tensor_reduce(neg_max[:], z[:, HALF:], mybir.AxisListType.X, ALU.max, negate=True)
 
         e_sb = keep.tile([P, S], F32, name="e_sb")
         total = keep.tile([P, 1], F32, name="total")
-        nc.scalar.activation(e_sb[:], z[:], ACT.Exp, bias=neg_max[:], scale=1.0, accum_out=total[:])
+        nc.scalar.activation(e_sb[:], z[:, :S], ACT.Exp, bias=neg_max[:], scale=1.0, accum_out=total[:])
         inv = keep.tile([P, 1], F32, name="inv")
         nc.vector.reciprocal(inv[:], total[:])
         for h, queue in enumerate((nc.sync, nc.scalar)):

@@ -29,14 +29,16 @@ def tile_picked_phrank_none_p_kernel(tc, x_words, x_scales, w1, prior, offs, out
         offsets = keep.tile([P, S // 16], U16, name="offsets")
 
         byte_table = keep.tile([P, T], U8, name="byte_table")
-        nc.vector.memset(byte_table[:].bitcast(I32), 0)
-        nc.sync.dma_start(byte_table[0:P:8, :].bitcast(I32), x_scales[0].bitcast(I32))
+        nc.vector.memset(byte_table[:].bitcast(I32)[:, :288], 0)
+        nc.gpsimd.memset(byte_table[:].bitcast(I32)[:, 288:], 0)
         nc.sync.dma_start(offsets[:], offs)
         plane = keep.tile([P, S], U8, name="plane", align_bytes=64)
         nc.vector.memset(plane[:].bitcast(I32), 0)
 
         w_raw = keep.tile([P, PACK, N], F32, name="w_raw")
         nc.sync.dma_start(w_raw[:], w1.rearrange("(p j) m -> p j m", j=PACK))
+
+        nc.sync.dma_start(byte_table[0:P:8, :].bitcast(I32), x_scales[0].bitcast(I32))
 
         word_table = keep.tile([P, T], I32, name="word_table")
         nc.sync.dma_start(word_table[:], x_words[0].rearrange("p c r -> p (c r)").bitcast(I32))
@@ -74,16 +76,16 @@ def tile_picked_phrank_none_p_kernel(tc, x_words, x_scales, w1, prior, offs, out
             )
             scores.append(acc)
 
-        z = keep.tile([P, S + 1], F32, name="z")
+        z = keep.tile([P, S], F32, name="z")
+        for h in range(2):
+            cols = slice(h * HALF, (h + 1) * HALF)
+            nc.vector.tensor_tensor(z[:, cols], scores[h][:], prior_sb[:, cols], ALU.add)
         neg_max = keep.tile([P, 1], F32, name="neg_max")
-        nc.vector.tensor_tensor(z[:, :HALF], scores[0][:], prior_sb[:, :HALF], ALU.add)
-        nc.vector.tensor_reduce(z[:, S:], z[:, :HALF], mybir.AxisListType.X, ALU.max)
-        nc.vector.tensor_tensor(z[:, HALF:S], scores[1][:], prior_sb[:, HALF:], ALU.add)
-        nc.vector.tensor_reduce(neg_max[:], z[:, HALF:], mybir.AxisListType.X, ALU.max, negate=True)
+        nc.vector.tensor_reduce(neg_max[:], z[:], mybir.AxisListType.X, ALU.max, negate=True)
 
         e_sb = keep.tile([P, S], F32, name="e_sb")
         total = keep.tile([P, 1], F32, name="total")
-        nc.scalar.activation(e_sb[:], z[:, :S], ACT.Exp, bias=neg_max[:], scale=1.0, accum_out=total[:])
+        nc.scalar.activation(e_sb[:], z[:], ACT.Exp, bias=neg_max[:], scale=1.0, accum_out=total[:])
         inv = keep.tile([P, 1], F32, name="inv")
         nc.vector.reciprocal(inv[:], total[:])
         for h, queue in enumerate((nc.sync, nc.scalar)):

@@ -18,6 +18,7 @@ ACT = mybir.ActivationFunctionType
 P = 128
 PACK = 4
 HALF = S // 2
+LEAD = 4
 
 
 def tile_picked_phrank_none_p_kernel(tc, x_words, x_scales, w1, prior, offs, out):
@@ -31,14 +32,15 @@ def tile_picked_phrank_none_p_kernel(tc, x_words, x_scales, w1, prior, offs, out
         byte_table = keep.tile([P, T], U8, name="byte_table")
         nc.vector.memset(byte_table[:].bitcast(I32)[:, :288], 0)
         nc.gpsimd.memset(byte_table[:].bitcast(I32)[:, 288:], 0)
-        nc.sync.dma_start(offsets[:], offs)
-        plane = keep.tile([P, S], U8, name="plane", align_bytes=64)
-        nc.vector.memset(plane[:].bitcast(I32), 0)
-
         w_raw = keep.tile([P, PACK, N], F32, name="w_raw")
         nc.sync.dma_start(w_raw[:], w1.rearrange("(p j) m -> p j m", j=PACK))
+        nc.sync.dma_start(offsets[:], offs)
+        planes = [keep.tile([P, HALF], U8, name=f"plane{h}", align_bytes=64) for h in range(2)]
+        nc.vector.memset(planes[0][:].bitcast(I32), 0)
 
-        nc.sync.dma_start(byte_table[0:P:8, :].bitcast(I32), x_scales[0].bitcast(I32))
+
+        for i in range(2):
+            nc.sync.dma_start(byte_table[i:P:16, :].bitcast(I32), x_scales[0, i:16:2, :].bitcast(I32))
 
         word_table = keep.tile([P, T], I32, name="word_table")
         nc.sync.dma_start(word_table[:], x_words[0].rearrange("p c r -> p (c r)").bitcast(I32))
@@ -49,11 +51,15 @@ def tile_picked_phrank_none_p_kernel(tc, x_words, x_scales, w1, prior, offs, out
         w_grouped = keep.tile([P, N, PACK], BF16, name="w_grouped", align_bytes=64)
         nc.scalar.copy(w_grouped[:], w_raw[:].rearrange("p j m -> p m j"))
 
-        picked_bytes = keep.tile([P, S], U8, name="picked_bytes", align_bytes=64)
-        nc.vector.tensor_copy(picked_bytes[:], byte_table[:].indirect(offsets[:]))
-        for q in range(4):
-            queue = nc.scalar if q % 2 else nc.sync
-            queue.dma_start(plane[32 * q : 32 * q + 4, :].bitcast(I32), picked_bytes[32 * q : 32 * q + 32 : 8, :].bitcast(I32))
+        for h in range(2):
+            cols = slice(h * HALF // 16, (h + 1) * HALF // 16)
+            picked_bytes = keep.tile([P, HALF], U8, name=f"picked_bytes{h}", align_bytes=64)
+            nc.vector.tensor_copy(picked_bytes[:], byte_table[:].indirect(offsets[:, cols]))
+            if h == 1:
+                nc.vector.tensor_copy(planes[h][:].bitcast(I32), picked_bytes[:].bitcast(I32))
+            for j in range(2 * h, 4):
+                queue = nc.scalar if j % 2 else nc.sync
+                queue.dma_start(planes[h][j:P:32, :].bitcast(I32), picked_bytes[16 * (j // 2) + j % 2 : P : 32, :].bitcast(I32))
 
         w_codes = keep.tile([P, N], U32, name="w_codes", align_bytes=64)
         w_scales = keep.tile([P, N], U8, name="w_scales", align_bytes=64)
@@ -70,22 +76,22 @@ def tile_picked_phrank_none_p_kernel(tc, x_words, x_scales, w1, prior, offs, out
                 lhsT=w_codes[:].bitcast(FP8X4),
                 lhsT_scale=w_scales[:],
                 rhs=picked_words[:].bitcast(FP8X4),
-                rhs_scale=plane[:, h * HALF : (h + 1) * HALF],
+                rhs_scale=planes[h][:],
                 start=True,
                 stop=True,
             )
             scores.append(acc)
 
-        z = keep.tile([P, S], F32, name="z")
-        for h in range(2):
-            cols = slice(h * HALF, (h + 1) * HALF)
-            nc.vector.tensor_tensor(z[:, cols], scores[h][:], prior_sb[:, cols], ALU.add)
+        z = keep.tile([P, 2, LEAD + HALF], F32, name="z")
+        nc.vector.tensor_tensor(z[:, 0, LEAD:], scores[0][:], prior_sb[:, :HALF], ALU.add)
+        nc.vector.tensor_reduce(z[:, 1, LEAD - 1 : LEAD], z[:, 0, LEAD:], mybir.AxisListType.X, ALU.max)
+        nc.vector.tensor_tensor(z[:, 1, LEAD:], scores[1][:], prior_sb[:, HALF:], ALU.add)
         neg_max = keep.tile([P, 1], F32, name="neg_max")
-        nc.vector.tensor_reduce(neg_max[:], z[:], mybir.AxisListType.X, ALU.max, negate=True)
+        nc.vector.tensor_reduce(neg_max[:], z[:, 1, LEAD - 1 :], mybir.AxisListType.X, ALU.max, negate=True)
 
         e_sb = keep.tile([P, S], F32, name="e_sb")
         total = keep.tile([P, 1], F32, name="total")
-        nc.scalar.activation(e_sb[:], z[:], ACT.Exp, bias=neg_max[:], scale=1.0, accum_out=total[:])
+        nc.scalar.activation(e_sb[:].rearrange("p (h c) -> p h c", h=2), z[:, :, LEAD:], ACT.Exp, bias=neg_max[:], scale=1.0, accum_out=total[:])
         inv = keep.tile([P, 1], F32, name="inv")
         nc.vector.reciprocal(inv[:], total[:])
         for h, queue in enumerate((nc.sync, nc.scalar)):

@@ -19,6 +19,7 @@ P = 128
 PACK = 4
 HALF = S // 2
 LEAD = 4
+EARLY = 384
 
 
 def tile_picked_phrank_none_p_kernel(tc, x_words, x_scales, w1, prior, offs, out):
@@ -35,6 +36,9 @@ def tile_picked_phrank_none_p_kernel(tc, x_words, x_scales, w1, prior, offs, out
         w_raw = keep.tile([P, PACK, N], F32, name="w_raw")
         nc.sync.dma_start(w_raw[:], w1.rearrange("(p j) m -> p j m", j=PACK))
         nc.sync.dma_start(offsets[:], offs)
+        word_table = keep.tile([P, T], I32, name="word_table")
+        words = x_words[0].rearrange("p c r -> p (c r)").bitcast(I32)
+        nc.sync.dma_start(word_table[:, :EARLY], words[:, :EARLY])
         planes = [keep.tile([P, HALF], U8, name=f"plane{h}", align_bytes=64) for h in range(2)]
         nc.vector.memset(planes[0][:].bitcast(I32), 0)
 
@@ -42,8 +46,7 @@ def tile_picked_phrank_none_p_kernel(tc, x_words, x_scales, w1, prior, offs, out
         for i in range(2):
             nc.sync.dma_start(byte_table[i:P:16, :].bitcast(I32), x_scales[0, i:16:2, :].bitcast(I32))
 
-        word_table = keep.tile([P, T], I32, name="word_table")
-        nc.sync.dma_start(word_table[:], x_words[0].rearrange("p c r -> p (c r)").bitcast(I32))
+        nc.sync.dma_start(word_table[:, EARLY:], words[:, EARLY:])
 
         prior_sb = keep.tile([P, S], F32, name="prior_sb")
         nc.sync.dma_start(prior_sb[:], prior)

@@ -18,6 +18,7 @@ ACT = mybir.ActivationFunctionType
 P = 128
 PACK = 4
 HALF = S // 2
+QUARTER = S // 4
 LEAD = 4
 EARLY = 384
 
@@ -30,7 +31,7 @@ def tile_picked_phrank_none_p_kernel(tc, x_words, x_scales, w1, prior, offs, out
 
         offsets = keep.tile([P, S // 16], U16, name="offsets")
 
-        byte_table = keep.tile([P, T], U8, name="byte_table")
+        byte_table = keep.tile([P, T], U8, name="byte_table", tag="byte_table", align_bytes=64)
         nc.vector.memset(byte_table[:].bitcast(I32)[:, :288], 0)
         nc.gpsimd.memset(byte_table[:].bitcast(I32)[:, 288:], 0)
         w_raw = keep.tile([P, PACK, N], F32, name="w_raw")
@@ -64,7 +65,7 @@ def tile_picked_phrank_none_p_kernel(tc, x_words, x_scales, w1, prior, offs, out
                 queue = nc.scalar if j % 2 else nc.sync
                 queue.dma_start(planes[h][j:P:32, :].bitcast(I32), picked_bytes[16 * (j // 2) + j % 2 : P : 32, :].bitcast(I32))
 
-        w_codes = keep.tile([P, N], U32, name="w_codes", align_bytes=64)
+        w_codes = keep.tile([P, N], U32, name="w_codes", tag="byte_table", align_bytes=64)
         w_scales = keep.tile([P, N], U8, name="w_scales", align_bytes=64)
         nc.vector.quantize_mx(out=w_codes[:].bitcast(FP8X4), scales=w_scales[:], in_=w_grouped[:].rearrange("p m j -> p (m j)"))
 
@@ -73,24 +74,39 @@ def tile_picked_phrank_none_p_kernel(tc, x_words, x_scales, w1, prior, offs, out
             cols = slice(h * HALF // 16, (h + 1) * HALF // 16)
             picked_words = keep.tile([P, HALF], U32, name=f"picked_words{h}", align_bytes=64)
             nc.vector.tensor_copy(picked_words[:], word_table[:].bitcast(U32).indirect(offsets[:, cols]))
-            acc = psum.tile([P, HALF], F32, name=f"acc{h}")
-            nc.tensor.matmul_mx(
-                out=acc[:],
-                lhsT=w_codes[:].bitcast(FP8X4),
-                lhsT_scale=w_scales[:],
-                rhs=picked_words[:].bitcast(FP8X4),
-                rhs_scale=planes[h][:],
-                start=True,
-                stop=True,
-            )
-            scores.append(acc)
+            width = HALF // (h + 1)
+            for c0 in range(0, HALF, width):
+                acc = psum.tile([P, width], F32, name=f"acc{h}_{c0}")
+                nc.tensor.matmul_mx(
+                    out=acc[:],
+                    lhsT=w_codes[:].bitcast(FP8X4),
+                    lhsT_scale=w_scales[:],
+                    rhs=picked_words[:, c0 : c0 + width].bitcast(FP8X4),
+                    rhs_scale=planes[h][:, c0 : c0 + width],
+                    start=True,
+                    stop=True,
+                )
+                scores.extend(acc[:, q0 : q0 + QUARTER] for q0 in range(0, width, QUARTER))
 
         z = keep.tile([P, 2, LEAD + HALF], F32, name="z")
-        nc.vector.tensor_tensor(z[:, 0, LEAD:], scores[0][:], prior_sb[:, :HALF], ALU.add)
-        nc.vector.tensor_reduce(z[:, 1, LEAD - 1 : LEAD], z[:, 0, LEAD:], mybir.AxisListType.X, ALU.max)
-        nc.vector.tensor_tensor(z[:, 1, LEAD:], scores[1][:], prior_sb[:, HALF:], ALU.add)
+
+        def quarter(q):
+            return z[:, q // 2, LEAD + q % 2 * QUARTER : LEAD + (q % 2 + 1) * QUARTER]
+
+        def add_prior(q):
+            nc.vector.tensor_tensor(quarter(q), scores[q], prior_sb[:, q * QUARTER : (q + 1) * QUARTER], ALU.add)
+
+        def quarter_max(q):
+            nc.vector.tensor_reduce(z[:, 1, LEAD - 2 + q : LEAD - 1 + q], quarter(q), mybir.AxisListType.X, ALU.max)
+
+        add_prior(0)
+        add_prior(1)
+        quarter_max(0)
+        add_prior(2)
+        quarter_max(1)
+        add_prior(3)
         neg_max = keep.tile([P, 1], F32, name="neg_max")
-        nc.vector.tensor_reduce(neg_max[:], z[:, 1, LEAD - 1 :], mybir.AxisListType.X, ALU.max, negate=True)
+        nc.vector.tensor_reduce(neg_max[:], z[:, 1, LEAD - 2 :], mybir.AxisListType.X, ALU.max, negate=True)
 
         e_sb = keep.tile([P, S], F32, name="e_sb")
         total = keep.tile([P, 1], F32, name="total")

@@ -32,8 +32,7 @@ def tile_picked_phrank_none_p_kernel(tc, x_words, x_scales, w1, prior, offs, out
         offsets = keep.tile([P, S // 16], U16, name="offsets")
 
         byte_table = keep.tile([P, T], U8, name="byte_table", tag="byte_table", align_bytes=64)
-        nc.vector.memset(byte_table[:].bitcast(I32)[:, :288], 0)
-        nc.gpsimd.memset(byte_table[:].bitcast(I32)[:, 288:], 0)
+        nc.vector.memset(byte_table[:].bitcast(I32), 0)
         w_raw = keep.tile([P, PACK, N], F32, name="w_raw")
         nc.sync.dma_start(w_raw[:], w1.rearrange("(p j) m -> p j m", j=PACK))
         nc.sync.dma_start(offsets[:], offs)
@@ -74,19 +73,18 @@ def tile_picked_phrank_none_p_kernel(tc, x_words, x_scales, w1, prior, offs, out
             cols = slice(h * HALF // 16, (h + 1) * HALF // 16)
             picked_words = keep.tile([P, HALF], U32, name=f"picked_words{h}", align_bytes=64)
             nc.vector.tensor_copy(picked_words[:], word_table[:].bitcast(U32).indirect(offsets[:, cols]))
-            width = HALF // (h + 1)
-            for c0 in range(0, HALF, width):
-                acc = psum.tile([P, width], F32, name=f"acc{h}_{c0}")
+            for c0 in range(0, HALF, QUARTER):
+                acc = psum.tile([P, QUARTER], F32, name=f"acc{h}_{c0}")
                 nc.tensor.matmul_mx(
                     out=acc[:],
                     lhsT=w_codes[:].bitcast(FP8X4),
                     lhsT_scale=w_scales[:],
-                    rhs=picked_words[:, c0 : c0 + width].bitcast(FP8X4),
-                    rhs_scale=planes[h][:, c0 : c0 + width],
+                    rhs=picked_words[:, c0 : c0 + QUARTER].bitcast(FP8X4),
+                    rhs_scale=planes[h][:, c0 : c0 + QUARTER],
                     start=True,
                     stop=True,
                 )
-                scores.extend(acc[:, q0 : q0 + QUARTER] for q0 in range(0, width, QUARTER))
+                scores.append(acc[:])
 
         z = keep.tile([P, 2, LEAD + HALF], F32, name="z")
 

@@ -17,6 +17,9 @@ ACT = mybir.ActivationFunctionType
 
 P = 128
 PACK = 4
+QUADRANT = 32
+BLOCK_ROWS = 8
+LIST_ROWS = 16
 HALF = S // 2
 QUARTER = S // 4
 LEAD = 4
@@ -29,23 +32,23 @@ def tile_picked_phrank_none_p_kernel(tc, x_words, x_scales, w1, prior, offs, out
         keep = ctx.enter_context(tc.tile_pool(name="keep", bufs=1))
         psum = ctx.enter_context(tc.psum_pool(name="psum", bufs=1))
 
-        offsets = keep.tile([P, S // 16], U16, name="offsets")
+        offsets = keep.tile([P, S // LIST_ROWS], U16, name="offsets")
 
         byte_table = keep.tile([P, T], U8, name="byte_table", tag="byte_table", align_bytes=64)
         nc.vector.memset(byte_table[:].bitcast(I32), 0)
+
         w_raw = keep.tile([P, PACK, N], F32, name="w_raw")
         nc.sync.dma_start(w_raw[:], w1.rearrange("(p j) m -> p j m", j=PACK))
         nc.sync.dma_start(offsets[:], offs)
+
         word_table = keep.tile([P, T], I32, name="word_table")
         words = x_words[0].rearrange("p c r -> p (c r)").bitcast(I32)
         nc.sync.dma_start(word_table[:, :EARLY], words[:, :EARLY])
+
         planes = [keep.tile([P, HALF], U8, name=f"plane{h}", align_bytes=64) for h in range(2)]
         nc.vector.memset(planes[0][:].bitcast(I32), 0)
 
-
-        for i in range(2):
-            nc.sync.dma_start(byte_table[i:P:16, :].bitcast(I32), x_scales[0, i:16:2, :].bitcast(I32))
-
+        nc.sync.dma_start(byte_table[0:P:BLOCK_ROWS, :].bitcast(I32), x_scales[0].bitcast(I32))
         nc.sync.dma_start(word_table[:, EARLY:], words[:, EARLY:])
 
         prior_sb = keep.tile([P, S], F32, name="prior_sb")
@@ -55,14 +58,19 @@ def tile_picked_phrank_none_p_kernel(tc, x_words, x_scales, w1, prior, offs, out
         nc.scalar.copy(w_grouped[:], w_raw[:].rearrange("p j m -> p m j"))
 
         for h in range(2):
-            cols = slice(h * HALF // 16, (h + 1) * HALF // 16)
+            entries = slice(h * HALF // LIST_ROWS, (h + 1) * HALF // LIST_ROWS)
             picked_bytes = keep.tile([P, HALF], U8, name=f"picked_bytes{h}", align_bytes=64)
-            nc.vector.tensor_copy(picked_bytes[:], byte_table[:].indirect(offsets[:, cols]))
+            nc.vector.tensor_copy(picked_bytes[:], byte_table[:].indirect(offsets[:, entries]))
+            first_moved = 0
             if h == 1:
                 nc.vector.tensor_copy(planes[h][:].bitcast(I32), picked_bytes[:].bitcast(I32))
-            for j in range(2 * h, 4):
+                first_moved = 1
+            for j in range(first_moved, QUADRANT // BLOCK_ROWS):
                 queue = nc.scalar if j % 2 else nc.sync
-                queue.dma_start(planes[h][j:P:32, :].bitcast(I32), picked_bytes[16 * (j // 2) + j % 2 : P : 32, :].bitcast(I32))
+                queue.dma_start(
+                    planes[h][j:P:QUADRANT, :].bitcast(I32),
+                    picked_bytes[BLOCK_ROWS * j : P : QUADRANT, :].bitcast(I32),
+                )
 
         w_codes = keep.tile([P, N], U32, name="w_codes", tag="byte_table", align_bytes=64)
         w_scales = keep.tile([P, N], U8, name="w_scales", align_bytes=64)
@@ -70,9 +78,9 @@ def tile_picked_phrank_none_p_kernel(tc, x_words, x_scales, w1, prior, offs, out
 
         scores = []
         for h in range(2):
-            cols = slice(h * HALF // 16, (h + 1) * HALF // 16)
+            entries = slice(h * HALF // LIST_ROWS, (h + 1) * HALF // LIST_ROWS)
             picked_words = keep.tile([P, HALF], U32, name=f"picked_words{h}", align_bytes=64)
-            nc.vector.tensor_copy(picked_words[:], word_table[:].bitcast(U32).indirect(offsets[:, cols]))
+            nc.vector.tensor_copy(picked_words[:], word_table[:].bitcast(U32).indirect(offsets[:, entries]))
             for c0 in range(0, HALF, QUARTER):
                 acc = psum.tile([P, QUARTER], F32, name=f"acc{h}_{c0}")
                 nc.tensor.matmul_mx(
@@ -88,14 +96,17 @@ def tile_picked_phrank_none_p_kernel(tc, x_words, x_scales, w1, prior, offs, out
 
         z = keep.tile([P, 2, LEAD + HALF], F32, name="z")
 
-        def quarter(q):
-            return z[:, q // 2, LEAD + q % 2 * QUARTER : LEAD + (q % 2 + 1) * QUARTER]
+        def z_quarter(quarter):
+            start = LEAD + quarter % 2 * QUARTER
+            return z[:, quarter // 2, start : start + QUARTER]
 
-        def add_prior(q):
-            nc.vector.tensor_tensor(quarter(q), scores[q], prior_sb[:, q * QUARTER : (q + 1) * QUARTER], ALU.add)
+        def add_prior(quarter):
+            cols = slice(quarter * QUARTER, (quarter + 1) * QUARTER)
+            nc.vector.tensor_tensor(z_quarter(quarter), scores[quarter], prior_sb[:, cols], ALU.add)
 
-        def quarter_max(q):
-            nc.vector.tensor_reduce(z[:, 1, LEAD - 2 + q : LEAD - 1 + q], quarter(q), mybir.AxisListType.X, ALU.max)
+        def quarter_max(quarter):
+            slot = LEAD - 2 + quarter
+            nc.vector.tensor_reduce(z[:, 1, slot : slot + 1], z_quarter(quarter), mybir.AxisListType.X, ALU.max)
 
         add_prior(0)
         add_prior(1)
@@ -111,6 +122,7 @@ def tile_picked_phrank_none_p_kernel(tc, x_words, x_scales, w1, prior, offs, out
         nc.scalar.activation(e_sb[:].rearrange("p (h c) -> p h c", h=2), z[:, :, LEAD:], ACT.Exp, bias=neg_max[:], scale=1.0, accum_out=total[:])
         inv = keep.tile([P, 1], F32, name="inv")
         nc.vector.reciprocal(inv[:], total[:])
+
         for h, queue in enumerate((nc.sync, nc.scalar)):
             cols = slice(h * HALF, (h + 1) * HALF)
             res = keep.tile([P, HALF], F32, name=f"res{h}")

@@ -23,7 +23,7 @@ LIST_ROWS = 16
 HALF = S // 2
 QUARTER = S // 4
 LEAD = 4
-EARLY = 384
+EARLY = 256
 
 
 def tile_picked_phrank_none_p_kernel(tc, x_words, x_scales, w1, prior, offs, out):

@@ -23,7 +23,7 @@ LIST_ROWS = 16
 HALF = S // 2
 QUARTER = S // 4
 LEAD = 4
-EARLY = 256
+EARLY = 128
 
 
 def tile_picked_phrank_none_p_kernel(tc, x_words, x_scales, w1, prior, offs, out):
@@ -48,7 +48,8 @@ def tile_picked_phrank_none_p_kernel(tc, x_words, x_scales, w1, prior, offs, out
         planes = [keep.tile([P, HALF], U8, name=f"plane{h}", align_bytes=64) for h in range(2)]
         nc.vector.memset(planes[0][:].bitcast(I32), 0)
 
-        nc.sync.dma_start(byte_table[0:P:BLOCK_ROWS, :].bitcast(I32), x_scales[0].bitcast(I32))
+        for i in range(2):
+            nc.sync.dma_start(byte_table[i:P:LIST_ROWS, :].bitcast(I32), x_scales[0, i::2, :].bitcast(I32))
         nc.sync.dma_start(word_table[:, EARLY:], words[:, EARLY:])
 
         prior_sb = keep.tile([P, S], F32, name="prior_sb")
@@ -64,12 +65,12 @@ def tile_picked_phrank_none_p_kernel(tc, x_words, x_scales, w1, prior, offs, out
             first_moved = 0
             if h == 1:
                 nc.vector.tensor_copy(planes[h][:].bitcast(I32), picked_bytes[:].bitcast(I32))
-                first_moved = 1
+                first_moved = 2
             for j in range(first_moved, QUADRANT // BLOCK_ROWS):
                 queue = nc.scalar if j % 2 else nc.sync
                 queue.dma_start(
                     planes[h][j:P:QUADRANT, :].bitcast(I32),
-                    picked_bytes[BLOCK_ROWS * j : P : QUADRANT, :].bitcast(I32),
+                    picked_bytes[LIST_ROWS * (j // 2) + j % 2 : P : QUADRANT, :].bitcast(I32),
                 )
 
         w_codes = keep.tile([P, N], U32, name="w_codes", tag="byte_table", align_bytes=64)

@@ -18,12 +18,14 @@ ACT = mybir.ActivationFunctionType
 P = 128
 PACK = 4
 QUADRANT = 32
-BLOCK_ROWS = 8
+QUADRANT_ROWS = 4
+RUN_ROWS = 2
 LIST_ROWS = 16
 HALF = S // 2
 QUARTER = S // 4
 LEAD = 4
 EARLY = 128
+VECTOR_SHARE = 384
 
 
 def tile_picked_phrank_none_p_kernel(tc, x_words, x_scales, w1, prior, offs, out):
@@ -48,8 +50,8 @@ def tile_picked_phrank_none_p_kernel(tc, x_words, x_scales, w1, prior, offs, out
         planes = [keep.tile([P, HALF], U8, name=f"plane{h}", align_bytes=64) for h in range(2)]
         nc.vector.memset(planes[0][:].bitcast(I32), 0)
 
-        for i in range(2):
-            nc.sync.dma_start(byte_table[i:P:LIST_ROWS, :].bitcast(I32), x_scales[0, i::2, :].bitcast(I32))
+        for i in range(RUN_ROWS):
+            nc.sync.dma_start(byte_table[i:P:LIST_ROWS, :].bitcast(I32), x_scales[0, i::RUN_ROWS, :].bitcast(I32))
         nc.sync.dma_start(word_table[:, EARLY:], words[:, EARLY:])
 
         prior_sb = keep.tile([P, S], F32, name="prior_sb")
@@ -65,12 +67,13 @@ def tile_picked_phrank_none_p_kernel(tc, x_words, x_scales, w1, prior, offs, out
             first_moved = 0
             if h == 1:
                 nc.vector.tensor_copy(planes[h][:].bitcast(I32), picked_bytes[:].bitcast(I32))
-                first_moved = 2
-            for j in range(first_moved, QUADRANT // BLOCK_ROWS):
+                first_moved = RUN_ROWS
+            for j in range(first_moved, QUADRANT_ROWS):
                 queue = nc.scalar if j % 2 else nc.sync
+                gathered_on = LIST_ROWS * (j // RUN_ROWS) + j % RUN_ROWS
                 queue.dma_start(
                     planes[h][j:P:QUADRANT, :].bitcast(I32),
-                    picked_bytes[LIST_ROWS * (j // 2) + j % 2 : P : QUADRANT, :].bitcast(I32),
+                    picked_bytes[gathered_on:P:QUADRANT, :].bitcast(I32),
                 )
 
         w_codes = keep.tile([P, N], U32, name="w_codes", tag="byte_table", align_bytes=64)
@@ -124,8 +127,7 @@ def tile_picked_phrank_none_p_kernel(tc, x_words, x_scales, w1, prior, offs, out
         inv = keep.tile([P, 1], F32, name="inv")
         nc.vector.reciprocal(inv[:], total[:])
 
-        for h, queue in enumerate((nc.sync, nc.scalar)):
-            cols = slice(h * HALF, (h + 1) * HALF)
-            res = keep.tile([P, HALF], F32, name=f"res{h}")
-            nc.vector.tensor_scalar(res[:], e_sb[:, cols], inv[:], None, ALU.mult)
-            queue.dma_start(out[:, cols], res[:])
+        res = keep.tile([P, S], F32, name="res")
+        nc.vector.tensor_scalar(res[:, :VECTOR_SHARE], e_sb[:, :VECTOR_SHARE], inv[:], None, ALU.mult)
+        nc.scalar.activation(res[:, VECTOR_SHARE:], e_sb[:, VECTOR_SHARE:], ACT.Copy, scale=inv[:])
+        nc.sync.dma_start(out, res[:])

@@ -24,7 +24,6 @@ LIST_ROWS = 16
 HALF = S // 2
 QUARTER = S // 4
 LEAD = 4
-EARLY = 128
 VECTOR_SHARE = 384
 
 
@@ -45,14 +44,15 @@ def tile_picked_phrank_none_p_kernel(tc, x_words, x_scales, w1, prior, offs, out
 
         word_table = keep.tile([P, T], I32, name="word_table")
         words = x_words[0].rearrange("p c r -> p (c r)").bitcast(I32)
-        nc.sync.dma_start(word_table[:, :EARLY], words[:, :EARLY])
 
         planes = [keep.tile([P, HALF], U8, name=f"plane{h}", align_bytes=64) for h in range(2)]
         nc.vector.memset(planes[0][:].bitcast(I32), 0)
 
         for i in range(RUN_ROWS):
             nc.sync.dma_start(byte_table[i:P:LIST_ROWS, :].bitcast(I32), x_scales[0, i::RUN_ROWS, :].bitcast(I32))
-        nc.sync.dma_start(word_table[:, EARLY:], words[:, EARLY:])
+        for half in range(2):
+            cols = slice(half * T // 2, (half + 1) * T // 2)
+            nc.sync.dma_start(word_table[:, cols], words[:, cols])
 
         prior_sb = keep.tile([P, S], F32, name="prior_sb")
         nc.sync.dma_start(prior_sb[:], prior)

@@ -49,7 +49,7 @@ def tile_picked_phrank_none_p_kernel(tc, x_words, x_scales, w1, prior, offs, out
         nc.vector.memset(planes[0][:].bitcast(I32), 0)
 
         for i in range(RUN_ROWS):
-            nc.sync.dma_start(byte_table[i:P:LIST_ROWS, :].bitcast(I32), x_scales[0, i::RUN_ROWS, :].bitcast(I32))
+            (nc.scalar if i else nc.sync).dma_start(byte_table[i:P:LIST_ROWS, :].bitcast(I32), x_scales[0, i::RUN_ROWS, :].bitcast(I32))
         for half in range(2):
             cols = slice(half * T // 2, (half + 1) * T // 2)
             nc.sync.dma_start(word_table[:, cols], words[:, cols])

@@ -24,7 +24,6 @@ LIST_ROWS = 16
 HALF = S // 2
 QUARTER = S // 4
 LEAD = 4
-VECTOR_SHARE = 384
 
 
 def tile_picked_phrank_none_p_kernel(tc, x_words, x_scales, w1, prior, offs, out):
@@ -128,6 +127,5 @@ def tile_picked_phrank_none_p_kernel(tc, x_words, x_scales, w1, prior, offs, out
         nc.vector.reciprocal(inv[:], total[:])
 
         res = keep.tile([P, S], F32, name="res")
-        nc.vector.tensor_scalar(res[:, :VECTOR_SHARE], e_sb[:, :VECTOR_SHARE], inv[:], None, ALU.mult)
-        nc.scalar.activation(res[:, VECTOR_SHARE:], e_sb[:, VECTOR_SHARE:], ACT.Copy, scale=inv[:])
+        nc.vector.tensor_scalar(res[:], e_sb[:], inv[:], None, ALU.mult)
         nc.sync.dma_start(out, res[:])

from contextlib import ExitStack

import concourse.mybir as mybir

K, T, S, N = 512, 2048, 512, 128
FLOPS = 2 * K * N * S

F32 = mybir.dt.float32
BF16 = mybir.dt.bfloat16
I32 = mybir.dt.int32
U32 = mybir.dt.uint32
U16 = mybir.dt.uint16
U8 = mybir.dt.uint8
FP8X4 = mybir.dt.float8_e4m3fn_x4
ALU = mybir.AluOpType
ACT = mybir.ActivationFunctionType

P = 128
PACK = 4
QUADRANT = 32
QUADRANT_ROWS = 4
RUN_ROWS = 2
LIST_ROWS = 16
HALF = S // 2
QUARTER = S // 4
LEAD = 4


def tile_picked_phrank_none_p_kernel(tc, x_words, x_scales, w1, prior, offs, out):
    nc = tc.nc
    with ExitStack() as ctx:
        keep = ctx.enter_context(tc.tile_pool(name="keep", bufs=1))
        psum = ctx.enter_context(tc.psum_pool(name="psum", bufs=1))

        offsets = keep.tile([P, S // LIST_ROWS], U16, name="offsets")

        byte_table = keep.tile([P, T], U8, name="byte_table", tag="byte_table", align_bytes=64)
        nc.vector.memset(byte_table[:].bitcast(I32), 0)

        w_raw = keep.tile([P, PACK, N], F32, name="w_raw")
        nc.sync.dma_start(w_raw[:], w1.rearrange("(p j) m -> p j m", j=PACK))
        nc.sync.dma_start(offsets[:], offs)

        word_table = keep.tile([P, T], I32, name="word_table")
        words = x_words[0].rearrange("p c r -> p (c r)").bitcast(I32)

        planes = [keep.tile([P, HALF], U8, name=f"plane{h}", align_bytes=64) for h in range(2)]
        nc.vector.memset(planes[0][:].bitcast(I32), 0)

        for i in range(RUN_ROWS):
            (nc.scalar if i else nc.sync).dma_start(byte_table[i:P:LIST_ROWS, :].bitcast(I32), x_scales[0, i::RUN_ROWS, :].bitcast(I32))
        for half in range(2):
            cols = slice(half * T // 2, (half + 1) * T // 2)
            nc.sync.dma_start(word_table[:, cols], words[:, cols])

        prior_sb = keep.tile([P, S], F32, name="prior_sb")
        nc.sync.dma_start(prior_sb[:], prior)

        w_grouped = keep.tile([P, N, PACK], BF16, name="w_grouped", align_bytes=64)
        nc.scalar.copy(w_grouped[:], w_raw[:].rearrange("p j m -> p m j"))

        for h in range(2):
            entries = slice(h * HALF // LIST_ROWS, (h + 1) * HALF // LIST_ROWS)
            picked_bytes = keep.tile([P, HALF], U8, name=f"picked_bytes{h}", align_bytes=64)
            nc.vector.tensor_copy(picked_bytes[:], byte_table[:].indirect(offsets[:, entries]))
            first_moved = 0
            if h == 1:
                nc.vector.tensor_copy(planes[h][:].bitcast(I32), picked_bytes[:].bitcast(I32))
                first_moved = RUN_ROWS
            for j in range(first_moved, QUADRANT_ROWS):
                queue = nc.scalar if j % 2 else nc.sync
                gathered_on = LIST_ROWS * (j // RUN_ROWS) + j % RUN_ROWS
                queue.dma_start(
                    planes[h][j:P:QUADRANT, :].bitcast(I32),
                    picked_bytes[gathered_on:P:QUADRANT, :].bitcast(I32),
                )

        w_codes = keep.tile([P, N], U32, name="w_codes", tag="byte_table", align_bytes=64)
        w_scales = keep.tile([P, N], U8, name="w_scales", align_bytes=64)
        nc.vector.quantize_mx(out=w_codes[:].bitcast(FP8X4), scales=w_scales[:], in_=w_grouped[:].rearrange("p m j -> p (m j)"))

        scores = []
        for h in range(2):
            entries = slice(h * HALF // LIST_ROWS, (h + 1) * HALF // LIST_ROWS)
            picked_words = keep.tile([P, HALF], U32, name=f"picked_words{h}", align_bytes=64)
            nc.vector.tensor_copy(picked_words[:], word_table[:].bitcast(U32).indirect(offsets[:, entries]))
            for c0 in range(0, HALF, QUARTER):
                acc = psum.tile([P, QUARTER], F32, name=f"acc{h}_{c0}")
                nc.tensor.matmul_mx(
                    out=acc[:],
                    lhsT=w_codes[:].bitcast(FP8X4),
                    lhsT_scale=w_scales[:],
                    rhs=picked_words[:, c0 : c0 + QUARTER].bitcast(FP8X4),
                    rhs_scale=planes[h][:, c0 : c0 + QUARTER],
                    start=True,
                    stop=True,
                )
                scores.append(acc[:])

        z = keep.tile([P, 2, LEAD + HALF], F32, name="z")

        def z_quarter(quarter):
            start = LEAD + quarter % 2 * QUARTER
            return z[:, quarter // 2, start : start + QUARTER]

        def add_prior(quarter):
            cols = slice(quarter * QUARTER, (quarter + 1) * QUARTER)
            nc.vector.tensor_tensor(z_quarter(quarter), scores[quarter], prior_sb[:, cols], ALU.add)

        def quarter_max(quarter):
            slot = LEAD - 2 + quarter
            nc.vector.tensor_reduce(z[:, 1, slot : slot + 1], z_quarter(quarter), mybir.AxisListType.X, ALU.max)

        add_prior(0)
        add_prior(1)
        quarter_max(0)
        add_prior(2)
        quarter_max(1)
        add_prior(3)
        neg_max = keep.tile([P, 1], F32, name="neg_max")
        nc.vector.tensor_reduce(neg_max[:], z[:, 1, LEAD - 2 :], mybir.AxisListType.X, ALU.max, negate=True)

        e_sb = keep.tile([P, S], F32, name="e_sb")
        total = keep.tile([P, 1], F32, name="total")
        nc.scalar.activation(e_sb[:].rearrange("p (h c) -> p h c", h=2), z[:, :, LEAD:], ACT.Exp, bias=neg_max[:], scale=1.0, accum_out=total[:])
        inv = keep.tile([P, 1], F32, name="inv")
        nc.vector.reciprocal(inv[:], total[:])

        res = keep.tile([P, S], F32, name="res")
        nc.vector.tensor_scalar(res[:], e_sb[:], inv[:], None, ALU.mult)
        nc.sync.dma_start(out, res[:])
